import numpy as np
import ml_dtypes


def mxq(x, axis, fmt="e4m3"):
    dtype, down = {"e4m3": (ml_dtypes.float8_e4m3fn, 7), "e5m2": (ml_dtypes.float8_e5m2, 14)}[fmt]
    v = np.moveaxis(np.asarray(x, np.float32).astype(ml_dtypes.bfloat16).astype(np.float64), axis, -1)
    blocks = v.reshape(v.shape[:-1] + (-1, 32))
    amax = np.abs(blocks).max(-1, keepdims=True)
    byte = np.maximum(np.where(amax > 0, np.frexp(amax)[1] - 1 + 127, 0) - down, 1)
    scale = np.exp2(byte - 127.0)
    codes = (blocks / scale).astype(np.float32).astype(dtype).astype(np.float64)
    return np.moveaxis((codes * scale).reshape(v.shape), -1, axis)


WIDE = False


def mx_kscale(k):
    if not WIDE:
        return np.ones(k)
    levels = np.array([10, -10, 5, -5, 0])
    if k % 512:
        return np.exp2(np.random.permutation(np.resize(levels, k // 32))).repeat(32)
    a = np.empty((k // 512, 16))
    for p in range(k // 512):
        a[p, :8] = np.random.permutation(np.resize(levels, 8))
        for g in range(8):
            far = levels[np.abs(levels - a[p, g]) >= 10]
            a[p, g + 8] = far[np.random.randint(len(far))]
    return np.exp2(a.ravel()).repeat(32)


def f64(x):
    return np.asarray(x).astype(np.float64)


def striped(idx):
    return np.tile(idx.reshape(-1, 16).T, (8, 1)).astype(np.uint16)


def unstriped(offs):
    return offs[:16].T.reshape(-1).astype(np.int64)


def pack_weight(w):
    k, n = w.shape
    w = f64(np.asarray(w, np.float32).astype(ml_dtypes.bfloat16)).reshape(k // 32, 32, n)
    amax = np.abs(w).max(1)
    byte = np.clip(np.where(amax > 0, np.frexp(amax)[1] - 1 + 127 - 7, 1), 1, 254)
    scaled = (w * np.exp2(127.0 - byte)[:, None, :]).reshape(k, n).astype(np.float32)
    words = np.ascontiguousarray(scaled.reshape(k // 512, 128, 4, n).transpose(0, 1, 3, 2)).astype(ml_dtypes.float8_e4m3fn).view(np.uint8)
    return words, np.ascontiguousarray(byte.astype(np.uint8).reshape(k // 512, 16, n))


def unpack_weight(words, scales):
    g, p, n, _ = words.shape
    vals = np.ascontiguousarray(words).view(ml_dtypes.float8_e4m3fn).astype(np.float64) * np.repeat(np.exp2(scales.astype(np.float64) - 127.0), 8, axis=1)[..., None]
    return vals.transpose(0, 1, 3, 2).reshape(g * 512, n)


def relu(v):
    return np.maximum(v, 0.0)


K, T, S, H, V, W = 1024, 1024, 512, 512, 512, 2048
P = 2 ** 7


def setup_inputs():
    n = np.random.standard_normal
    s = mx_kscale(K)[:, None]
    u = mx_kscale(H)
    packed_xT = pack_weight(n((K, T)) * s)
    packed_eT = pack_weight(n((H, W)) / np.sqrt(H) / u[:, None])
    return {
        "x_words": packed_xT[0],
        "x_scales": packed_xT[1],
        "w1": (n((K, H)) / np.sqrt(K) / s * u).astype(np.float32),
        "e_words": packed_eT[0],
        "e_scales": packed_eT[1],
        "inv": (np.tile(np.random.uniform(0.7, 1.3, W), (P, 1))).astype(np.float32),
        "own": (np.random.uniform(0.7, 1.3, (S, 1))).astype(np.float32),
        "prob": (np.random.uniform(0.1, 1.0, (S, 1))).astype(np.float32),
        "offs": striped(np.random.permutation(T)[:S]),
        "hist": striped(np.random.permutation(W)[:V]),
    }


def reference(x_words, x_scales, w1, e_words, e_scales, inv, own, prob, offs, hist):
    xq = unpack_weight(x_words, x_scales)[:, unstriped(offs)]
    h = mxq(f64(w1), 0, "e4m3").T @ xq
    e_hist = unpack_weight(e_words, e_scales)[:, unstriped(hist)]
    y = f64(own) * ((0.2 * ((mxq(h, 0, "e4m3").T @ e_hist))) * (f64(inv)[:1][:, unstriped(hist)]))
    pen = y.max(axis=1, keepdims=True)
    score = -0.6 * pen + f64(prob)
    return relu(2.0 * y + score)

@@ -1,0 +1,224 @@
+from contextlib import ExitStack
+
+import concourse.mybir as mybir
+from concourse.masks import make_identity
+
+K, T, S, H, V, W = 1024, 1024, 512, 512, 512, 2048
+FLOPS = 2 * K * H * S + 2 * H * S * V
+BYTES = K * T + K * T // 32 + 4 * K * H + H * W + H * W // 32 + 4 * W + 8 * S + 2 * 128 * 64 + 4 * S * V
+
+F32 = mybir.dt.float32
+BF16 = mybir.dt.bfloat16
+I32 = mybir.dt.int32
+U32 = mybir.dt.uint32
+U16 = mybir.dt.uint16
+U8 = mybir.dt.uint8
+FP8X4 = mybir.dt.float8_e4m3fn_x4
+ALU = mybir.AluOpType
+ACT = mybir.ActivationFunctionType
+
+P = 128
+PACK = 4
+PASSES = K // (P * PACK)
+CHUNKS = S // P
+QUADS = 4
+
+
+def tile_picked_ycsrch_rel_p_kernel(
+    tc, x_words, x_scales, w1, e_words, e_scales, inv, own, prob, offs, hist, out
+):
+    nc = tc.nc
+    with ExitStack() as ctx:
+        keep = ctx.enter_context(tc.tile_pool(name="keep", bufs=1))
+        reuse = ctx.enter_context(tc.tile_pool(name="reuse", bufs=1))
+        psum = ctx.enter_context(tc.psum_pool(name="psum", bufs=4))
+
+        def at(offset, name, shape, dtype):
+            return reuse.tile(shape, dtype, name=name, align_bytes=64, offset=offset)
+
+        def sb(name, shape, dtype):
+            return keep.tile(shape, dtype, name=name, align_bytes=64)
+
+        offs_sb = sb("offs_sb", [P, S // 16], U16)
+        hist_sb = sb("hist_sb", [P, V // 16], U16)
+        xs_all = sb("xs_all", [P, T], U8)
+        es_all = sb("es_all", [P, W], U8)
+        inv_all = sb("inv_all", [P, W], F32)
+        xw_all = [sb(f"xw_all{o}", [P, T], U32) for o in range(PASSES)]
+        ew_all = at(0, "ew_all", [P, W], U32)
+        w_raw = [at(8192 * (o + 1), f"w_raw{o}", [P, PACK, H], F32) for o in range(PASSES)]
+        rows = sb("rows", [P, P], F32)
+        ident = sb("ident", [P, P], F32)
+
+        nc.vector.memset(xs_all[:].bitcast(I32), 0)
+        nc.vector.memset(inv_all[:], 0.0)
+        nc.vector.memset(es_all[:].bitcast(I32), 0)
+
+        def load_w(o):
+            nc.sync.dma_start(
+                out=w_raw[o][:],
+                in_=w1[o * P * PACK : (o + 1) * P * PACK, :].rearrange("(p j) c -> p j c", j=PACK),
+            )
+
+        def load_words(dst, src):
+            nc.sync.dma_start(out=dst[:].bitcast(I32), in_=src.rearrange("p n r -> p (n r)").bitcast(I32))
+
+        nc.sync.dma_start(offs_sb[:], offs)
+        load_words(xw_all[0], x_words[0])
+        for q in range(QUADS):
+            nc.sync.dma_start(
+                out=xs_all[32 * q : 32 * q + 4 * PASSES, :].bitcast(I32),
+                in_=x_scales[:, 4 * q : 4 * q + 4, :].bitcast(I32),
+            )
+        load_w(0)
+        nc.sync.dma_start(hist_sb[:], hist)
+        nc.sync.dma_start(out=inv_all[0:1, :], in_=inv[0:1, :])
+        for q in range(QUADS):
+            nc.sync.dma_start(
+                out=es_all[32 * q : 32 * q + 4, :].bitcast(I32),
+                in_=e_scales[0, 4 * q : 4 * q + 4, :].bitcast(I32),
+            )
+        load_w(1)
+        load_words(xw_all[1], x_words[1])
+        load_words(ew_all, e_words[0])
+
+        make_identity(nc, ident[:])
+        nc.gpsimd.memset(rows[:], 0.0)
+        nc.gpsimd.dma_start(out=rows[0:CHUNKS, :], in_=own.rearrange("(c p) one -> c (p one)", p=P))
+        nc.gpsimd.dma_start(out=rows[CHUNKS : 2 * CHUNKS, :], in_=prob.rearrange("(c p) one -> c (p one)", p=P))
+
+        xw0 = sb("xw0", [P, S], U32)
+        nc.vector.tensor_copy(xw0[:], xw_all[0][:].indirect(offs_sb[:]))
+        xs = sb("xs", [P, S], U8)
+        nc.vector.tensor_copy(xs[:], xs_all[:].indirect(offs_sb[:]))
+        inv_row = sb("inv_row", [P, V], F32)
+        nc.vector.tensor_copy(inv_row[:], inv_all[:].indirect(hist_sb[:]))
+        es = sb("es", [P, V], U8)
+        nc.vector.tensor_copy(es[:], es_all[:].indirect(hist_sb[:]))
+
+        w_bf = [sb(f"w_bf{o}", [P, PACK, P, PACK], BF16) for o in range(PASSES)]
+        w_codes = [sb(f"w_codes{o}", [P, H], U32) for o in range(PASSES)]
+        w_scales = [sb(f"w_scales{o}", [P, H], U8) for o in range(PASSES)]
+
+        def deal_views(o, m0, m1):
+            dst = w_bf[o][:, :, m0:m1, :].rearrange("p t m j -> p m j t")
+            src = w_raw[o][:].rearrange("p j (m t) -> p m j t", t=PACK)[:, m0:m1, :, :]
+            return dst, src
+
+        def quantise_w(o):
+            nc.vector.quantize_mx(
+                out=w_codes[o][:].bitcast(FP8X4),
+                scales=w_scales[o][:],
+                in_=w_bf[o][:].rearrange("p t m j -> p (t m j)"),
+            )
+
+        dst, src = deal_views(0, 0, P)
+        nc.scalar.activation(dst, src, ACT.Copy)
+        dst, src = deal_views(1, 0, P // 2)
+        nc.scalar.activation(dst, src, ACT.Copy)
+        dst, src = deal_views(1, P // 2, P)
+        nc.vector.tensor_copy(dst, src)
+        quantise_w(0)
+
+        cuts = [0, 2 * P, 3 * P, 4 * P]
+        xw1 = [sb("xw1_0", [P, 2 * P], U32), sb("xw1_1", [P, P], U32), at(4096, "xw1_2", [P, P], U32)]
+
+        def gather_x1(u):
+            nc.vector.tensor_copy(xw1[u][:], xw_all[1][:].indirect(offs_sb[:, cuts[u] // 16 : cuts[u + 1] // 16]))
+
+        gather_x1(0)
+        quantise_w(1)
+        gather_x1(1)
+
+        turned = psum.tile([P, CHUNKS, P], F32, name="turned", tag="s")
+        for c in range(CHUNKS):
+            nc.tensor.transpose(turned[:, c, :], inv_row[:, c * P : (c + 1) * P], ident[:])
+        inv_col = sb("inv_col", [P, CHUNKS], F32)
+        nc.scalar.activation(inv_col[:], turned[:, :, 0], ACT.Copy, scale=0.4)
+        spread = psum.tile([P, V], F32, name="spread", tag="s")
+        for c in range(CHUNKS):
+            nc.tensor.transpose(spread[:, c * P : (c + 1) * P], inv_col[:, c : c + 1].to_broadcast([P, P]), ident[:])
+        inv_b = at(8192 * 2, "inv_b", [P, V], F32)
+        nc.scalar.activation(inv_b[:], spread[:], ACT.Copy)
+        cols_ps = psum.tile([P, P], F32, name="cols_ps", tag="s")
+        nc.tensor.transpose(cols_ps[:], rows[:], ident[:])
+        cols = sb("cols", [P, 2 * CHUNKS], F32)
+        nc.scalar.activation(cols[:], cols_ps[:, 0 : 2 * CHUNKS], ACT.Copy)
+
+        def x_operand(o, c):
+            if o == 0:
+                return xw0[:, c * P : (c + 1) * P]
+            if c < 2:
+                return xw1[0][:, c * P : (c + 1) * P]
+            return xw1[c - 1][:]
+
+        h_codes = [at(512 * c, f"h_codes{c}", [P, P], U32) for c in range(CHUNKS)]
+        h_scales = [sb(f"h_scales{c}", [P, P], U8) for c in range(CHUNKS)]
+        h_bf = [sb(f"h_bf{c}", [P, P, PACK], BF16) for c in range(CHUNKS)]
+
+        def project(c):
+            h_ps = psum.tile([P, PACK, P], F32, name=f"h_ps{c}", tag="h")
+            for t in range(PACK):
+                for o in range(PASSES):
+                    nc.tensor.matmul_mx(
+                        out=h_ps[:, t, :],
+                        lhsT=w_codes[o][:, t * P : (t + 1) * P].bitcast(FP8X4),
+                        lhsT_scale=w_scales[o][:, t * P : (t + 1) * P],
+                        rhs=x_operand(o, c).bitcast(FP8X4),
+                        rhs_scale=xs[4 * o : P, c * P : (c + 1) * P],
+                        start=(o == 0),
+                        stop=(o == PASSES - 1),
+                    )
+            nc.scalar.activation(h_bf[c][:], h_ps[:].rearrange("p t s -> p s t"), ACT.Copy)
+
+        def quantise_h(c):
+            nc.vector.quantize_mx(
+                out=h_codes[c][:].bitcast(FP8X4),
+                scales=h_scales[c][:],
+                in_=h_bf[c][:].rearrange("p s t -> p (s t)"),
+            )
+
+        s_ps = [None] * CHUNKS
+        ew = sb("ew", [P, V], U32)
+
+        def score_product(c):
+            s_ps[c] = psum.tile([P, V], F32, name=f"s_ps{c}", tag="s")
+            nc.tensor.matmul_mx(
+                out=s_ps[c][:],
+                lhsT=h_codes[c][:].bitcast(FP8X4),
+                lhsT_scale=h_scales[c][:],
+                rhs=ew[:].bitcast(FP8X4),
+                rhs_scale=es[:],
+                start=True,
+                stop=True,
+            )
+
+        def finish(c):
+            y2 = sb(f"y2_{c}", [P, V], F32)
+            nc.vector.scalar_tensor_tensor(y2[:], s_ps[c][:], cols[:, c : c + 1], inv_b[:], ALU.mult, ALU.mult)
+            top = sb(f"top{c}", [P, 1], F32)
+            nc.vector.tensor_reduce(top[:], y2[:], mybir.AxisListType.X, ALU.max)
+            score = sb(f"score{c}", [P, 1], F32)
+            nc.scalar.activation(score[:], top[:], ACT.Identity, bias=cols[:, CHUNKS + c : CHUNKS + c + 1], scale=-0.3)
+            res = sb(f"res{c}", [P, V], F32)
+            nc.scalar.activation(res[:], y2[:], ACT.Relu, bias=score[:], scale=1.0)
+            nc.sync.dma_start(out=out[c * P : (c + 1) * P, :], in_=res[:])
+
+        project(0)
+        project(1)
+        project(2)
+        nc.vector.tensor_copy(ew[:], ew_all[:].indirect(hist_sb[:]))
+        quantise_h(0)
+        score_product(0)
+        gather_x1(2)
+        quantise_h(1)
+        score_product(1)
+        project(3)
+        finish(0)
+        quantise_h(2)
+        score_product(2)
+        finish(1)
+        quantise_h(3)
+        score_product(3)
+        finish(2)
+        finish(3)

@@ -39,20 +39,21 @@ def tile_picked_ycsrch_rel_p_kernel(
         def sb(name, shape, dtype):
             return keep.tile(shape, dtype, name=name, align_bytes=64)
 
+        E_AT, W_AT, B_AT, X_AT = 0, 8192, 16384, 20480
         offs_sb = sb("offs_sb", [P, S // 16], U16)
         hist_sb = sb("hist_sb", [P, V // 16], U16)
         xs_all = sb("xs_all", [P, T], U8)
         es_all = sb("es_all", [P, W], U8)
         inv_all = sb("inv_all", [P, W], F32)
-        xw_all = [sb(f"xw_all{o}", [P, T], U32) for o in range(PASSES)]
-        ew_all = at(0, "ew_all", [P, W], U32)
-        w_raw = [at(8192 * (o + 1), f"w_raw{o}", [P, PACK, H], F32) for o in range(PASSES)]
-        rows = sb("rows", [P, P], F32)
+        xw_all = [sb("xw_all0", [P, T], U32), at(X_AT, "xw_all1", [P, T], U32)]
+        ew_all = at(E_AT, "ew_all", [P, W], U32)
+        w_raw = [sb("w_raw0", [P, PACK, H], F32), at(W_AT, "w_raw1", [P, PACK, H], F32)]
         ident = sb("ident", [P, P], F32)
+        rows = sb("rows", [P, P], F32)
 
         nc.vector.memset(xs_all[:].bitcast(I32), 0)
         nc.vector.memset(inv_all[:], 0.0)
-        nc.vector.memset(es_all[:].bitcast(I32), 0)
+        nc.gpsimd.memset(es_all[:].bitcast(I32), 0)
 
         def load_w(o):
             nc.sync.dma_start(
@@ -87,23 +88,16 @@ def tile_picked_ycsrch_rel_p_kernel(
         nc.gpsimd.dma_start(out=rows[0:CHUNKS, :], in_=own.rearrange("(c p) one -> c (p one)", p=P))
         nc.gpsimd.dma_start(out=rows[CHUNKS : 2 * CHUNKS, :], in_=prob.rearrange("(c p) one -> c (p one)", p=P))
 
-        xw0 = sb("xw0", [P, S], U32)
-        nc.vector.tensor_copy(xw0[:], xw_all[0][:].indirect(offs_sb[:]))
-        xs = sb("xs", [P, S], U8)
-        nc.vector.tensor_copy(xs[:], xs_all[:].indirect(offs_sb[:]))
-        inv_row = sb("inv_row", [P, V], F32)
-        nc.vector.tensor_copy(inv_row[:], inv_all[:].indirect(hist_sb[:]))
-        es = sb("es", [P, V], U8)
-        nc.vector.tensor_copy(es[:], es_all[:].indirect(hist_sb[:]))
-
-        w_bf = [sb(f"w_bf{o}", [P, PACK, P, PACK], BF16) for o in range(PASSES)]
+        w_bf = [sb("w_bf0", [P, PACK, P, PACK], BF16), at(B_AT, "w_bf1", [P, PACK, P, PACK], BF16)]
         w_codes = [sb(f"w_codes{o}", [P, H], U32) for o in range(PASSES)]
         w_scales = [sb(f"w_scales{o}", [P, H], U8) for o in range(PASSES)]
 
-        def deal_views(o, m0, m1):
-            dst = w_bf[o][:, :, m0:m1, :].rearrange("p t m j -> p m j t")
-            src = w_raw[o][:].rearrange("p j (m t) -> p m j t", t=PACK)[:, m0:m1, :, :]
-            return dst, src
+        def deal_w(o):
+            nc.scalar.activation(
+                w_bf[o][:].rearrange("p t m j -> p m j t"),
+                w_raw[o][:].rearrange("p j (m t) -> p m j t", t=PACK),
+                ACT.Copy,
+            )
 
         def quantise_w(o):
             nc.vector.quantize_mx(
@@ -112,20 +106,28 @@ def tile_picked_ycsrch_rel_p_kernel(
                 in_=w_bf[o][:].rearrange("p t m j -> p (t m j)"),
             )
 
-        dst, src = deal_views(0, 0, P)
-        nc.scalar.activation(dst, src, ACT.Copy)
-        dst, src = deal_views(1, 0, P // 2)
-        nc.scalar.activation(dst, src, ACT.Copy)
-        dst, src = deal_views(1, P // 2, P)
-        nc.vector.tensor_copy(dst, src)
-        quantise_w(0)
-
-        cuts = [0, 2 * P, 3 * P, 4 * P]
-        xw1 = [sb("xw1_0", [P, 2 * P], U32), sb("xw1_1", [P, P], U32), at(4096, "xw1_2", [P, P], U32)]
+        half = S // 2
+        xw0 = sb("xw0", [P, S], U32)
+        xw1 = [sb("xw1_0", [P, half], U32), at(B_AT, "xw1_1", [P, half], U32)]
 
         def gather_x1(u):
-            nc.vector.tensor_copy(xw1[u][:], xw_all[1][:].indirect(offs_sb[:, cuts[u] // 16 : cuts[u + 1] // 16]))
+            nc.vector.tensor_copy(xw1[u][:], xw_all[1][:].indirect(offs_sb[:, u * half // 16 : (u + 1) * half // 16]))
 
+        def x_operand(o, c):
+            if o == 0:
+                return xw0[:, c * P : (c + 1) * P]
+            return xw1[c // 2][:, (c % 2) * P : (c % 2 + 1) * P]
+
+        nc.vector.tensor_copy(xw0[:], xw_all[0][:].indirect(offs_sb[:]))
+        xs = sb("xs", [P, S], U8)
+        nc.vector.tensor_copy(xs[:], xs_all[:].indirect(offs_sb[:]))
+        inv_row = sb("inv_row", [P, V], F32)
+        nc.vector.tensor_copy(inv_row[:], inv_all[:].indirect(hist_sb[:]))
+        es = sb("es", [P, V], U8)
+        nc.vector.tensor_copy(es[:], es_all[:].indirect(hist_sb[:]))
+        deal_w(0)
+        quantise_w(0)
+        deal_w(1)
         gather_x1(0)
         quantise_w(1)
         gather_x1(1)
@@ -134,25 +136,21 @@ def tile_picked_ycsrch_rel_p_kernel(
         for c in range(CHUNKS):
             nc.tensor.transpose(turned[:, c, :], inv_row[:, c * P : (c + 1) * P], ident[:])
         inv_col = sb("inv_col", [P, CHUNKS], F32)
-        nc.scalar.activation(inv_col[:], turned[:, :, 0], ACT.Copy, scale=0.4)
+        nc.vector.tensor_scalar(inv_col[:], turned[:, :, 0], -0.12, None, ALU.mult)
         spread = psum.tile([P, V], F32, name="spread", tag="s")
         for c in range(CHUNKS):
             nc.tensor.transpose(spread[:, c * P : (c + 1) * P], inv_col[:, c : c + 1].to_broadcast([P, P]), ident[:])
-        inv_b = at(8192 * 2, "inv_b", [P, V], F32)
+        inv_b = at(W_AT, "inv_b", [P, V], F32)
         nc.scalar.activation(inv_b[:], spread[:], ACT.Copy)
         cols_ps = psum.tile([P, P], F32, name="cols_ps", tag="s")
         nc.tensor.transpose(cols_ps[:], rows[:], ident[:])
-        cols = sb("cols", [P, 2 * CHUNKS], F32)
-        nc.scalar.activation(cols[:], cols_ps[:, 0 : 2 * CHUNKS], ACT.Copy)
+        cols = at(W_AT + 2048, "cols", [P, 2 * CHUNKS], F32)
+        own_col = cols[:, 0:CHUNKS]
+        prob_col = cols[:, CHUNKS : 2 * CHUNKS]
+        nc.scalar.activation(own_col, cols_ps[:, 0:CHUNKS], ACT.Copy)
+        nc.scalar.activation(prob_col, cols_ps[:, CHUNKS : 2 * CHUNKS], ACT.Copy, scale=-0.6 / 1.4)
 
-        def x_operand(o, c):
-            if o == 0:
-                return xw0[:, c * P : (c + 1) * P]
-            if c < 2:
-                return xw1[0][:, c * P : (c + 1) * P]
-            return xw1[c - 1][:]
-
-        h_codes = [at(512 * c, f"h_codes{c}", [P, P], U32) for c in range(CHUNKS)]
+        h_codes = [at(E_AT + 512 * c, f"h_codes{c}", [P, P], U32) for c in range(CHUNKS)]
         h_scales = [sb(f"h_scales{c}", [P, P], U8) for c in range(CHUNKS)]
         h_bf = [sb(f"h_bf{c}", [P, P, PACK], BF16) for c in range(CHUNKS)]
 
@@ -179,7 +177,7 @@ def tile_picked_ycsrch_rel_p_kernel(
             )
 
         s_ps = [None] * CHUNKS
-        ew = sb("ew", [P, V], U32)
+        ew = at(X_AT, "ew", [P, V], U32)
 
         def score_product(c):
             s_ps[c] = psum.tile([P, V], F32, name=f"s_ps{c}", tag="s")
@@ -193,32 +191,46 @@ def tile_picked_ycsrch_rel_p_kernel(
                 stop=True,
             )
 
-        def finish(c):
-            y2 = sb(f"y2_{c}", [P, V], F32)
-            nc.vector.scalar_tensor_tensor(y2[:], s_ps[c][:], cols[:, c : c + 1], inv_b[:], ALU.mult, ALU.mult)
-            top = sb(f"top{c}", [P, 1], F32)
-            nc.vector.tensor_reduce(top[:], y2[:], mybir.AxisListType.X, ALU.max)
-            score = sb(f"score{c}", [P, 1], F32)
-            nc.scalar.activation(score[:], top[:], ACT.Identity, bias=cols[:, CHUNKS + c : CHUNKS + c + 1], scale=-0.3)
-            res = sb(f"res{c}", [P, V], F32)
-            nc.scalar.activation(res[:], y2[:], ACT.Relu, bias=score[:], scale=1.0)
-            nc.sync.dma_start(out=out[c * P : (c + 1) * P, :], in_=res[:])
+        y2 = [sb(f"y2_{c}", [P, V], F32) for c in range(CHUNKS)]
 
+        def weigh(c):
+            nc.vector.scalar_tensor_tensor(y2[c][:], s_ps[c][:], own_col[:, c : c + 1], inv_b[:], ALU.mult, ALU.mult)
+
+        def finish(c):
+            shifted = sb(f"shifted{c}", [P, V], F32)
+            least = sb(f"least{c}", [P, 1], F32)
+            nc.vector.tensor_scalar(
+                shifted[:], y2[c][:], prob_col[:, c : c + 1], None, ALU.add, ALU.min, accum_out=least[:]
+            )
+            pieces = 2 if c == CHUNKS - 1 else 1
+            width = V // pieces
+            for u in range(pieces):
+                res = sb(f"res{c}_{u}", [P, width], F32)
+                span = slice(u * width, (u + 1) * width)
+                nc.scalar.activation(res[:], shifted[:, span], ACT.Relu, bias=least[:], scale=-2.0 / 0.6)
+                nc.sync.dma_start(out=out[c * P : (c + 1) * P, span], in_=res[:])
+
+        warm = psum.tile([P, S], F32, name="warm", tag="s")
+        for t in range(3):
+            nc.tensor.matmul_mx(
+                out=warm[:],
+                lhsT=w_codes[0][:, t * P : (t + 1) * P].bitcast(FP8X4),
+                lhsT_scale=w_scales[0][:, t * P : (t + 1) * P],
+                rhs=xw0[:].bitcast(FP8X4),
+                rhs_scale=xs[:],
+                start=True,
+                stop=True,
+            )
         project(0)
         project(1)
-        project(2)
         nc.vector.tensor_copy(ew[:], ew_all[:].indirect(hist_sb[:]))
-        quantise_h(0)
-        score_product(0)
-        gather_x1(2)
-        quantise_h(1)
-        score_product(1)
-        project(3)
-        finish(0)
-        quantise_h(2)
-        score_product(2)
-        finish(1)
-        quantise_h(3)
-        score_product(3)
-        finish(2)
-        finish(3)
+        for c in range(2):
+            quantise_h(c)
+            score_product(c)
+        for c in range(2, CHUNKS):
+            project(c)
+            quantise_h(c)
+            score_product(c)
+        for c in range(CHUNKS):
+            weigh(c)
+            finish(c)

@@ -74,11 +74,8 @@ def tile_picked_ycsrch_rel_p_kernel(
         load_w(0)
         nc.sync.dma_start(hist_sb[:], hist)
         nc.sync.dma_start(out=inv_all[0:1, :], in_=inv[0:1, :])
-        for q in range(QUADS):
-            nc.sync.dma_start(
-                out=es_all[32 * q : 32 * q + 4, :].bitcast(I32),
-                in_=e_scales[0, 4 * q : 4 * q + 4, :].bitcast(I32),
-            )
+        for r in range(4):
+            nc.sync.dma_start(out=es_all[r:P:32, :].bitcast(I32), in_=e_scales[0, r:16:4, :].bitcast(I32))
         load_w(1)
         load_words(xw_all[1], x_words[1])
         load_words(ew_all, e_words[0])
@@ -88,23 +85,33 @@ def tile_picked_ycsrch_rel_p_kernel(
         nc.gpsimd.dma_start(out=rows[0:CHUNKS, :], in_=own.rearrange("(c p) one -> c (p one)", p=P))
         nc.gpsimd.dma_start(out=rows[CHUNKS : 2 * CHUNKS, :], in_=prob.rearrange("(c p) one -> c (p one)", p=P))
 
-        w_bf = [sb("w_bf0", [P, PACK, P, PACK], BF16), at(B_AT, "w_bf1", [P, PACK, P, PACK], BF16)]
-        w_codes = [sb(f"w_codes{o}", [P, H], U32) for o in range(PASSES)]
-        w_scales = [sb(f"w_scales{o}", [P, H], U8) for o in range(PASSES)]
+        pieces_w = [(0, 0, 4), (1, 0, 2), (1, 2, 4)]
+        w_bf = [
+            sb("w_bf0", [P, 4, P, PACK], BF16),
+            sb("w_bf1", [P, 2, P, PACK], BF16),
+            at(B_AT, "w_bf2", [P, 2, P, PACK], BF16),
+        ]
+        w_codes = [sb(f"w_codes{n}", [P, (t1 - t0) * P], U32) for n, (o, t0, t1) in enumerate(pieces_w)]
+        w_scales = [sb(f"w_scales{n}", [P, (t1 - t0) * P], U8) for n, (o, t0, t1) in enumerate(pieces_w)]
 
-        def deal_w(o):
+        def deal_w(n):
+            o, t0, t1 = pieces_w[n]
             nc.scalar.activation(
-                w_bf[o][:].rearrange("p t m j -> p m j t"),
-                w_raw[o][:].rearrange("p j (m t) -> p m j t", t=PACK),
+                w_bf[n][:].rearrange("p t m j -> p m j t"),
+                w_raw[o][:].rearrange("p j (m t) -> p m j t", t=PACK)[:, :, :, t0:t1],
                 ACT.Copy,
             )
 
-        def quantise_w(o):
+        def quantise_w(n):
             nc.vector.quantize_mx(
-                out=w_codes[o][:].bitcast(FP8X4),
-                scales=w_scales[o][:],
-                in_=w_bf[o][:].rearrange("p t m j -> p (t m j)"),
+                out=w_codes[n][:].bitcast(FP8X4),
+                scales=w_scales[n][:],
+                in_=w_bf[n][:].rearrange("p t m j -> p (t m j)"),
             )
+
+        def w_operand(tiles, o, t):
+            n, first = (0, 0) if o == 0 else (1 + t // 2, t - t % 2)
+            return tiles[n][:, (t - first) * P : (t - first + 1) * P]
 
         half = S // 2
         xw0 = sb("xw0", [P, S], U32)
@@ -128,8 +135,10 @@ def tile_picked_ycsrch_rel_p_kernel(
         deal_w(0)
         quantise_w(0)
         deal_w(1)
+        deal_w(2)
         gather_x1(0)
         quantise_w(1)
+        quantise_w(2)
         gather_x1(1)
 
         turned = psum.tile([P, CHUNKS, P], F32, name="turned", tag="s")
@@ -150,7 +159,7 @@ def tile_picked_ycsrch_rel_p_kernel(
         nc.scalar.activation(own_col, cols_ps[:, 0:CHUNKS], ACT.Copy)
         nc.scalar.activation(prob_col, cols_ps[:, CHUNKS : 2 * CHUNKS], ACT.Copy, scale=-0.6 / 1.4)
 
-        h_codes = [at(E_AT + 512 * c, f"h_codes{c}", [P, P], U32) for c in range(CHUNKS)]
+        h_codes = [at(X_AT + 2048 if c == 0 else E_AT + 512 * c, f"h_codes{c}", [P, P], U32) for c in range(CHUNKS)]
         h_scales = [sb(f"h_scales{c}", [P, P], U8) for c in range(CHUNKS)]
         h_bf = [sb(f"h_bf{c}", [P, P, PACK], BF16) for c in range(CHUNKS)]
 
@@ -160,8 +169,8 @@ def tile_picked_ycsrch_rel_p_kernel(
                 for o in range(PASSES):
                     nc.tensor.matmul_mx(
                         out=h_ps[:, t, :],
-                        lhsT=w_codes[o][:, t * P : (t + 1) * P].bitcast(FP8X4),
-                        lhsT_scale=w_scales[o][:, t * P : (t + 1) * P],
+                        lhsT=w_operand(w_codes, o, t).bitcast(FP8X4),
+                        lhsT_scale=w_operand(w_scales, o, t),
                         rhs=x_operand(o, c).bitcast(FP8X4),
                         rhs_scale=xs[4 * o : P, c * P : (c + 1) * P],
                         start=(o == 0),
@@ -181,15 +190,21 @@ def tile_picked_ycsrch_rel_p_kernel(
 
         def score_product(c):
             s_ps[c] = psum.tile([P, V], F32, name=f"s_ps{c}", tag="s")
-            nc.tensor.matmul_mx(
-                out=s_ps[c][:],
-                lhsT=h_codes[c][:].bitcast(FP8X4),
-                lhsT_scale=h_scales[c][:],
-                rhs=ew[:].bitcast(FP8X4),
-                rhs_scale=es[:],
-                start=True,
-                stop=True,
-            )
+            width = V // 2 if c == 0 else V
+            for v0 in range(0, V, width):
+                nc.tensor.matmul_mx(
+                    out=s_ps[c][:, v0 : v0 + width],
+                    lhsT=h_codes[c][:].bitcast(FP8X4),
+                    lhsT_scale=h_scales[c][:],
+                    rhs=ew[:, v0 : v0 + width].bitcast(FP8X4),
+                    rhs_scale=es[:, v0 : v0 + width],
+                    start=True,
+                    stop=True,
+                )
+
+        def gather_e(u):
+            v0, v1 = u * V // 2, (u + 1) * V // 2
+            nc.vector.tensor_copy(ew[:, v0:v1], ew_all[:].indirect(hist_sb[:, v0 // 16 : v1 // 16]))
 
         y2 = [sb(f"y2_{c}", [P, V], F32) for c in range(CHUNKS)]
 
@@ -210,25 +225,14 @@ def tile_picked_ycsrch_rel_p_kernel(
                 nc.scalar.activation(res[:], shifted[:, span], ACT.Relu, bias=least[:], scale=-2.0 / 0.6)
                 nc.sync.dma_start(out=out[c * P : (c + 1) * P, span], in_=res[:])
 
-        warm = psum.tile([P, S], F32, name="warm", tag="s")
-        for t in range(3):
-            nc.tensor.matmul_mx(
-                out=warm[:],
-                lhsT=w_codes[0][:, t * P : (t + 1) * P].bitcast(FP8X4),
-                lhsT_scale=w_scales[0][:, t * P : (t + 1) * P],
-                rhs=xw0[:].bitcast(FP8X4),
-                rhs_scale=xs[:],
-                start=True,
-                stop=True,
-            )
-        project(0)
-        project(1)
-        nc.vector.tensor_copy(ew[:], ew_all[:].indirect(hist_sb[:]))
-        for c in range(2):
-            quantise_h(c)
-            score_product(c)
-        for c in range(2, CHUNKS):
+        for c in range(CHUNKS - 1):
             project(c)
+        gather_e(0)
+        quantise_h(0)
+        gather_e(1)
+        score_product(0)
+        project(CHUNKS - 1)
+        for c in range(1, CHUNKS):
             quantise_h(c)
             score_product(c)
         for c in range(CHUNKS):

@@ -53,7 +53,7 @@ def tile_picked_ycsrch_rel_p_kernel(
 
         nc.vector.memset(xs_all[:].bitcast(I32), 0)
         nc.vector.memset(inv_all[:], 0.0)
-        nc.gpsimd.memset(es_all[:].bitcast(I32), 0)
+        nc.vector.memset(es_all[:].bitcast(I32), 0)
 
         def load_w(o):
             nc.sync.dma_start(
@@ -211,6 +211,11 @@ def tile_picked_ycsrch_rel_p_kernel(
         def weigh(c):
             nc.vector.scalar_tensor_tensor(y2[c][:], s_ps[c][:], own_col[:, c : c + 1], inv_b[:], ALU.mult, ALU.mult)
 
+        def weigh_aside(c):
+            part = sb(f"part{c}", [P, V], F32)
+            nc.scalar.activation(part[:], s_ps[c][:], ACT.Copy, scale=own_col[:, c : c + 1])
+            nc.gpsimd.tensor_tensor(y2[c][:], part[:], inv_b[:], ALU.mult)
+
         def finish(c):
             shifted = sb(f"shifted{c}", [P, V], F32)
             least = sb(f"least{c}", [P, 1], F32)
@@ -235,6 +240,11 @@ def tile_picked_ycsrch_rel_p_kernel(
         for c in range(1, CHUNKS):
             quantise_h(c)
             score_product(c)
-        for c in range(CHUNKS):
-            weigh(c)
-            finish(c)
+        weigh(0)
+        weigh_aside(1)
+        finish(0)
+        weigh(2)
+        finish(2)
+        weigh(3)
+        finish(1)
+        finish(3)

from contextlib import ExitStack

import concourse.mybir as mybir
from concourse.masks import make_identity

K, T, S, H, V, W = 1024, 1024, 512, 512, 512, 2048
FLOPS = 2 * K * H * S + 2 * H * S * V
BYTES = K * T + K * T // 32 + 4 * K * H + H * W + H * W // 32 + 4 * W + 8 * S + 2 * 128 * 64 + 4 * S * V

F32 = mybir.dt.float32
BF16 = mybir.dt.bfloat16
I32 = mybir.dt.int32
U32 = mybir.dt.uint32
U16 = mybir.dt.uint16
U8 = mybir.dt.uint8
FP8X4 = mybir.dt.float8_e4m3fn_x4
ALU = mybir.AluOpType
ACT = mybir.ActivationFunctionType

P = 128
PACK = 4
PASSES = K // (P * PACK)
CHUNKS = S // P
QUADS = 4


def tile_picked_ycsrch_rel_p_kernel(
    tc, x_words, x_scales, w1, e_words, e_scales, inv, own, prob, offs, hist, out
):
    nc = tc.nc
    with ExitStack() as ctx:
        keep = ctx.enter_context(tc.tile_pool(name="keep", bufs=1))
        reuse = ctx.enter_context(tc.tile_pool(name="reuse", bufs=1))
        psum = ctx.enter_context(tc.psum_pool(name="psum", bufs=4))

        def at(offset, name, shape, dtype):
            return reuse.tile(shape, dtype, name=name, align_bytes=64, offset=offset)

        def sb(name, shape, dtype):
            return keep.tile(shape, dtype, name=name, align_bytes=64)

        E_AT, W_AT, B_AT, X_AT = 0, 8192, 16384, 20480
        offs_sb = sb("offs_sb", [P, S // 16], U16)
        hist_sb = sb("hist_sb", [P, V // 16], U16)
        xs_all = sb("xs_all", [P, T], U8)
        es_all = sb("es_all", [P, W], U8)
        inv_all = sb("inv_all", [P, W], F32)
        xw_all = [sb("xw_all0", [P, T], U32), at(X_AT, "xw_all1", [P, T], U32)]
        ew_all = at(E_AT, "ew_all", [P, W], U32)
        w_raw = [sb("w_raw0", [P, PACK, H], F32), at(W_AT, "w_raw1", [P, PACK, H], F32)]
        ident = sb("ident", [P, P], F32)
        rows = sb("rows", [P, P], F32)

        nc.vector.memset(xs_all[:].bitcast(I32), 0)
        nc.vector.memset(inv_all[:], 0.0)
        nc.vector.memset(es_all[:].bitcast(I32), 0)

        def load_w(o):
            nc.sync.dma_start(
                out=w_raw[o][:],
                in_=w1[o * P * PACK : (o + 1) * P * PACK, :].rearrange("(p j) c -> p j c", j=PACK),
            )

        def load_words(dst, src):
            nc.sync.dma_start(out=dst[:].bitcast(I32), in_=src.rearrange("p n r -> p (n r)").bitcast(I32))

        nc.sync.dma_start(offs_sb[:], offs)
        load_words(xw_all[0], x_words[0])
        for q in range(QUADS):
            nc.sync.dma_start(
                out=xs_all[32 * q : 32 * q + 4 * PASSES, :].bitcast(I32),
                in_=x_scales[:, 4 * q : 4 * q + 4, :].bitcast(I32),
            )
        load_w(0)
        nc.sync.dma_start(hist_sb[:], hist)
        nc.sync.dma_start(out=inv_all[0:1, :], in_=inv[0:1, :])
        for r in range(4):
            nc.sync.dma_start(out=es_all[r:P:32, :].bitcast(I32), in_=e_scales[0, r:16:4, :].bitcast(I32))
        load_w(1)
        load_words(xw_all[1], x_words[1])
        load_words(ew_all, e_words[0])

        make_identity(nc, ident[:])
        nc.gpsimd.memset(rows[:], 0.0)
        nc.gpsimd.dma_start(out=rows[0:CHUNKS, :], in_=own.rearrange("(c p) one -> c (p one)", p=P))
        nc.gpsimd.dma_start(out=rows[CHUNKS : 2 * CHUNKS, :], in_=prob.rearrange("(c p) one -> c (p one)", p=P))

        pieces_w = [(0, 0, 4), (1, 0, 2), (1, 2, 4)]
        w_bf = [
            sb("w_bf0", [P, 4, P, PACK], BF16),
            sb("w_bf1", [P, 2, P, PACK], BF16),
            at(B_AT, "w_bf2", [P, 2, P, PACK], BF16),
        ]
        w_codes = [sb(f"w_codes{n}", [P, (t1 - t0) * P], U32) for n, (o, t0, t1) in enumerate(pieces_w)]
        w_scales = [sb(f"w_scales{n}", [P, (t1 - t0) * P], U8) for n, (o, t0, t1) in enumerate(pieces_w)]

        def deal_w(n):
            o, t0, t1 = pieces_w[n]
            nc.scalar.activation(
                w_bf[n][:].rearrange("p t m j -> p m j t"),
                w_raw[o][:].rearrange("p j (m t) -> p m j t", t=PACK)[:, :, :, t0:t1],
                ACT.Copy,
            )

        def quantise_w(n):
            nc.vector.quantize_mx(
                out=w_codes[n][:].bitcast(FP8X4),
                scales=w_scales[n][:],
                in_=w_bf[n][:].rearrange("p t m j -> p (t m j)"),
            )

        def w_operand(tiles, o, t):
            n, first = (0, 0) if o == 0 else (1 + t // 2, t - t % 2)
            return tiles[n][:, (t - first) * P : (t - first + 1) * P]

        half = S // 2
        xw0 = sb("xw0", [P, S], U32)
        xw1 = [sb("xw1_0", [P, half], U32), at(B_AT, "xw1_1", [P, half], U32)]

        def gather_x1(u):
            nc.vector.tensor_copy(xw1[u][:], xw_all[1][:].indirect(offs_sb[:, u * half // 16 : (u + 1) * half // 16]))

        def x_operand(o, c):
            if o == 0:
                return xw0[:, c * P : (c + 1) * P]
            return xw1[c // 2][:, (c % 2) * P : (c % 2 + 1) * P]

        nc.vector.tensor_copy(xw0[:], xw_all[0][:].indirect(offs_sb[:]))
        xs = sb("xs", [P, S], U8)
        nc.vector.tensor_copy(xs[:], xs_all[:].indirect(offs_sb[:]))
        inv_row = sb("inv_row", [P, V], F32)
        nc.vector.tensor_copy(inv_row[:], inv_all[:].indirect(hist_sb[:]))
        es = sb("es", [P, V], U8)
        nc.vector.tensor_copy(es[:], es_all[:].indirect(hist_sb[:]))
        deal_w(0)
        quantise_w(0)
        deal_w(1)
        deal_w(2)
        gather_x1(0)
        quantise_w(1)
        quantise_w(2)
        gather_x1(1)

        turned = psum.tile([P, CHUNKS, P], F32, name="turned", tag="s")
        for c in range(CHUNKS):
            nc.tensor.transpose(turned[:, c, :], inv_row[:, c * P : (c + 1) * P], ident[:])
        inv_col = sb("inv_col", [P, CHUNKS], F32)
        nc.vector.tensor_scalar(inv_col[:], turned[:, :, 0], -0.12, None, ALU.mult)
        spread = psum.tile([P, V], F32, name="spread", tag="s")
        for c in range(CHUNKS):
            nc.tensor.transpose(spread[:, c * P : (c + 1) * P], inv_col[:, c : c + 1].to_broadcast([P, P]), ident[:])
        inv_b = at(W_AT, "inv_b", [P, V], F32)
        nc.scalar.activation(inv_b[:], spread[:], ACT.Copy)
        cols_ps = psum.tile([P, P], F32, name="cols_ps", tag="s")
        nc.tensor.transpose(cols_ps[:], rows[:], ident[:])
        cols = at(W_AT + 2048, "cols", [P, 2 * CHUNKS], F32)
        own_col = cols[:, 0:CHUNKS]
        prob_col = cols[:, CHUNKS : 2 * CHUNKS]
        nc.scalar.activation(own_col, cols_ps[:, 0:CHUNKS], ACT.Copy)
        nc.scalar.activation(prob_col, cols_ps[:, CHUNKS : 2 * CHUNKS], ACT.Copy, scale=-0.6 / 1.4)

        h_codes = [at(X_AT + 2048 if c == 0 else E_AT + 512 * c, f"h_codes{c}", [P, P], U32) for c in range(CHUNKS)]
        h_scales = [sb(f"h_scales{c}", [P, P], U8) for c in range(CHUNKS)]
        h_bf = [sb(f"h_bf{c}", [P, P, PACK], BF16) for c in range(CHUNKS)]

        def project(c):
            h_ps = psum.tile([P, PACK, P], F32, name=f"h_ps{c}", tag="h")
            for t in range(PACK):
                for o in range(PASSES):
                    nc.tensor.matmul_mx(
                        out=h_ps[:, t, :],
                        lhsT=w_operand(w_codes, o, t).bitcast(FP8X4),
                        lhsT_scale=w_operand(w_scales, o, t),
                        rhs=x_operand(o, c).bitcast(FP8X4),
                        rhs_scale=xs[4 * o : P, c * P : (c + 1) * P],
                        start=(o == 0),
                        stop=(o == PASSES - 1),
                    )
            nc.scalar.activation(h_bf[c][:], h_ps[:].rearrange("p t s -> p s t"), ACT.Copy)

        def quantise_h(c):
            nc.vector.quantize_mx(
                out=h_codes[c][:].bitcast(FP8X4),
                scales=h_scales[c][:],
                in_=h_bf[c][:].rearrange("p s t -> p (s t)"),
            )

        s_ps = [None] * CHUNKS
        ew = at(X_AT, "ew", [P, V], U32)

        def score_product(c):
            s_ps[c] = psum.tile([P, V], F32, name=f"s_ps{c}", tag="s")
            width = V // 2 if c == 0 else V
            for v0 in range(0, V, width):
                nc.tensor.matmul_mx(
                    out=s_ps[c][:, v0 : v0 + width],
                    lhsT=h_codes[c][:].bitcast(FP8X4),
                    lhsT_scale=h_scales[c][:],
                    rhs=ew[:, v0 : v0 + width].bitcast(FP8X4),
                    rhs_scale=es[:, v0 : v0 + width],
                    start=True,
                    stop=True,
                )

        def gather_e(u):
            v0, v1 = u * V // 2, (u + 1) * V // 2
            nc.vector.tensor_copy(ew[:, v0:v1], ew_all[:].indirect(hist_sb[:, v0 // 16 : v1 // 16]))

        y2 = [sb(f"y2_{c}", [P, V], F32) for c in range(CHUNKS)]

        def weigh(c):
            nc.vector.scalar_tensor_tensor(y2[c][:], s_ps[c][:], own_col[:, c : c + 1], inv_b[:], ALU.mult, ALU.mult)

        def weigh_aside(c):
            part = sb(f"part{c}", [P, V], F32)
            nc.scalar.activation(part[:], s_ps[c][:], ACT.Copy, scale=own_col[:, c : c + 1])
            nc.gpsimd.tensor_tensor(y2[c][:], part[:], inv_b[:], ALU.mult)

        def finish(c):
            shifted = sb(f"shifted{c}", [P, V], F32)
            least = sb(f"least{c}", [P, 1], F32)
            nc.vector.tensor_scalar(
                shifted[:], y2[c][:], prob_col[:, c : c + 1], None, ALU.add, ALU.min, accum_out=least[:]
            )
            pieces = 2 if c == CHUNKS - 1 else 1
            width = V // pieces
            for u in range(pieces):
                res = sb(f"res{c}_{u}", [P, width], F32)
                span = slice(u * width, (u + 1) * width)
                nc.scalar.activation(res[:], shifted[:, span], ACT.Relu, bias=least[:], scale=-2.0 / 0.6)
                nc.sync.dma_start(out=out[c * P : (c + 1) * P, span], in_=res[:])

        for c in range(CHUNKS - 1):
            project(c)
        gather_e(0)
        quantise_h(0)
        gather_e(1)
        score_product(0)
        project(CHUNKS - 1)
        for c in range(1, CHUNKS):
            quantise_h(c)
            score_product(c)
        weigh(0)
        weigh_aside(1)
        finish(0)
        weigh(2)
        finish(2)
        weigh(3)
        finish(1)
        finish(3)
